import numpy as np
import ml_dtypes


def mxq(x, axis, fmt="e4m3"):
    dtype, down = {"e4m3": (ml_dtypes.float8_e4m3fn, 7), "e5m2": (ml_dtypes.float8_e5m2, 14)}[fmt]
    v = np.moveaxis(np.asarray(x, np.float32).astype(ml_dtypes.bfloat16).astype(np.float64), axis, -1)
    blocks = v.reshape(v.shape[:-1] + (-1, 32))
    amax = np.abs(blocks).max(-1, keepdims=True)
    byte = np.maximum(np.where(amax > 0, np.frexp(amax)[1] - 1 + 127, 0) - down, 1)
    scale = np.exp2(byte - 127.0)
    codes = (blocks / scale).astype(np.float32).astype(dtype).astype(np.float64)
    return np.moveaxis((codes * scale).reshape(v.shape), -1, axis)


WIDE = False


def mx_kscale(k):
    if not WIDE:
        return np.ones(k)
    levels = np.array([10, -10, 5, -5, 0])
    if k % 512:
        return np.exp2(np.random.permutation(np.resize(levels, k // 32))).repeat(32)
    a = np.empty((k // 512, 16))
    for p in range(k // 512):
        a[p, :8] = np.random.permutation(np.resize(levels, 8))
        for g in range(8):
            far = levels[np.abs(levels - a[p, g]) >= 10]
            a[p, g + 8] = far[np.random.randint(len(far))]
    return np.exp2(a.ravel()).repeat(32)


def f64(x):
    return np.asarray(x).astype(np.float64)


def striped(idx):
    return np.tile(idx.reshape(-1, 16).T, (8, 1)).astype(np.uint16)


def unstriped(offs):
    return offs[:16].T.reshape(-1).astype(np.int64)


def striped8(idx):
    return np.concatenate([x.reshape(-1, 16).T for x in idx]).astype(np.uint16)


def runs(offs, k):
    lists = np.stack([offs[16 * r : 16 * r + 16].T.reshape(-1) for r in range(8)]).astype(np.int64)
    return lists[np.arange(k) % 512 // 64]


def pack_weight(w):
    k, n = w.shape
    w = f64(np.asarray(w, np.float32).astype(ml_dtypes.bfloat16)).reshape(k // 32, 32, n)
    amax = np.abs(w).max(1)
    byte = np.clip(np.where(amax > 0, np.frexp(amax)[1] - 1 + 127 - 7, 1), 1, 254)
    scaled = (w * np.exp2(127.0 - byte)[:, None, :]).reshape(k, n).astype(np.float32)
    words = np.ascontiguousarray(scaled.reshape(k // 512, 128, 4, n).transpose(0, 1, 3, 2)).astype(ml_dtypes.float8_e4m3fn).view(np.uint8)
    return words, np.ascontiguousarray(byte.astype(np.uint8).reshape(k // 512, 16, n))


def unpack_weight(words, scales):
    g, p, n, _ = words.shape
    vals = np.ascontiguousarray(words).view(ml_dtypes.float8_e4m3fn).astype(np.float64) * np.repeat(np.exp2(scales.astype(np.float64) - 127.0), 8, axis=1)[..., None]
    return vals.transpose(0, 1, 3, 2).reshape(g * 512, n)


def sigmoid(v):
    return 1.0 / (1.0 + np.exp(-np.maximum(v, -700.0)))


K, T, S, N, H = 512, 2048, 512, 512, 512


def setup_inputs():
    n = np.random.standard_normal
    s = mx_kscale(K)[:, None]
    u = mx_kscale(H)
    packed_xT = pack_weight(n((K, T)) * s)
    return {
        "x_words": packed_xT[0],
        "x_scales": packed_xT[1],
        "w1": (n((K, H)) / np.sqrt(K) / s).astype(np.float32),
        "gn": (np.random.uniform(0.5, 1.5, (H, 1)) * u[:, None]).astype(np.float32),
        "gm": (np.random.uniform(0.5, 1.5, (H, 1)) * u[:, None]).astype(np.float32),
        "w2": (n((H, N)) / np.sqrt(2 * H) / u[:, None]).astype(np.float32),
        "w3": (n((H, N)) / np.sqrt(2 * H) / u[:, None]).astype(np.float32),
        "offs": striped(np.random.permutation(T)[:S]),
        "n1": striped8(np.stack([np.random.permutation(S) for _ in range(8)])),
        "n2": striped8(np.stack([np.random.permutation(S) for _ in range(8)])),
        "n3": striped8(np.stack([np.random.permutation(S) for _ in range(8)])),
        "n4": striped8(np.stack([np.random.permutation(S) for _ in range(8)])),
    }


def reference(x_words, x_scales, w1, gn, gm, w2, w3, offs, n1, n2, n3, n4):
    xq = unpack_weight(x_words, x_scales)[:, unstriped(offs)]
    y = mxq(f64(w1), 0, "e4m3").T @ xq
    z = f64(gn) * (y * (sigmoid(y[np.arange(H)[:, None], runs(n1, H)])))
    ex = np.exp(y)
    z2 = f64(gm) * (np.log(ex + ex[np.arange(H)[:, None], runs(n2, H)]) - (y[np.arange(H)[:, None], runs(n3, H)]))
    h = mxq(f64(w2), 0, "e4m3").T @ mxq(z, 0, "e4m3") + mxq(f64(w3), 0, "e4m3").T @ mxq(z2, 0, "e4m3")
    pa = h[np.arange(N)[:, None], runs(n4, N)]
    return (2.0 * (h * pa)) / ((h) ** 2 + (pa) ** 2 + 0.5)

@@ -1,0 +1,183 @@
+from contextlib import ExitStack
+
+import concourse.mybir as mybir
+
+K, T, S, N, H = 512, 2048, 512, 512, 512
+FLOPS = 2 * K * H * S + 2 * 2 * H * N * S
+
+F32 = mybir.dt.float32
+BF16 = mybir.dt.bfloat16
+I32 = mybir.dt.int32
+U32 = mybir.dt.uint32
+U16 = mybir.dt.uint16
+U8 = mybir.dt.uint8
+FP8X4 = mybir.dt.float8_e4m3fn_x4
+ACT = mybir.ActivationFunctionType
+ALU = mybir.AluOpType
+
+P = 128
+PACK = 4
+WIN = 2 * S
+
+
+def tile_picked_joingatelseharm_none_p_kernel(tc, x_words, x_scales, w1, gn, gm, w2, w3, offs, n1, n2, n3, n4, out):
+    nc = tc.nc
+    with ExitStack() as ctx:
+        keep = ctx.enter_context(tc.tile_pool(name="keep", bufs=1))
+        psum = ctx.enter_context(tc.psum_pool(name="psum", bufs=1))
+
+        def new(name, shape, dtype):
+            return keep.tile(shape, dtype, name=name, align_bytes=64)
+
+        def load_list(name, src):
+            dst = keep.tile([P, S // 16], U16, name=name)
+            nc.sync.dma_start(dst[:], src)
+            return dst
+
+        def load_weight(name, w):
+            raw = new(name, [P, PACK, 512], F32)
+            nc.sync.dma_start(raw[:], w.rearrange("(p j) c -> p j c", j=PACK))
+            return raw
+
+        def load_gain(name, g):
+            dst = new(name, [P, PACK], F32)
+            nc.sync.dma_start(dst[:], g.rearrange("(p t) o -> p (t o)", t=PACK))
+            return dst
+
+        def group_weight(name, raw, shares):
+            grouped = new(name, [P, PACK * 512], BF16)
+            dst = grouped[:].rearrange("p (t m j) -> p m j t", t=PACK, j=PACK)
+            src = raw[:].rearrange("p j (m t) -> p m j t", t=PACK)
+            for copy, lo, hi in shares:
+                copy(dst[:, lo:hi], src[:, lo:hi])
+            return grouped
+
+        def group_values(name, planes, shares):
+            grouped = new(name, [P, PACK * S], BF16)
+            dst = grouped[:].rearrange("p (c i t) -> p c t i", t=PACK, i=4)
+            src = planes[:].rearrange("p t (c i) -> p c t i", i=4)
+            for copy, lo, hi in shares:
+                copy(dst[:, lo:hi], src[:, lo:hi])
+            return grouped
+
+        def quantize(name, grouped):
+            codes = new(name + "_codes", [P, 512], U32)
+            scales = new(name + "_scales", [P, 512], U8)
+            nc.vector.quantize_mx(out=codes[:].bitcast(FP8X4), scales=scales[:], in_=grouped[:])
+            return codes, scales
+
+        def product(bank, weight, t, moving, start, stop):
+            cols = slice(t * P, (t + 1) * P)
+            nc.tensor.matmul_mx(
+                out=bank[:], lhsT=weight[0][:, cols].bitcast(FP8X4), lhsT_scale=weight[1][:, cols],
+                rhs=moving[0][:].bitcast(FP8X4), rhs_scale=moving[1][:], start=start, stop=stop,
+            )
+
+        tiles = range(PACK)
+
+        on_vector, on_scalar = nc.vector.tensor_copy, nc.scalar.copy
+        last = PACK - 1
+        quarters = "p (a b) -> p a b"
+
+        xs_all = new("xs_all", [P, T], U8)
+        nc.vector.memset(xs_all[:].bitcast(I32), 0)
+        w1_raw = load_weight("w1_raw", w1)
+        offs_t = load_list("offs_t", offs)
+        for q in range(4):
+            nc.sync.dma_start(xs_all[32 * q : 32 * q + 4, :].bitcast(I32), x_scales[0, 4 * q : 4 * q + 4, :].bitcast(I32))
+        xw_all = new("xw_all", [P, T], I32)
+        nc.sync.dma_start(xw_all[:], x_words[0].rearrange("p n r -> p (n r)").bitcast(I32))
+        w2_raw = load_weight("w2_raw", w2)
+        w3_raw = load_weight("w3_raw", w3)
+        n2_t = load_list("n2_t", n2)
+        n1_t = load_list("n1_t", n1)
+        gn_t = load_gain("gn_t", gn)
+        gm_t = load_gain("gm_t", gm)
+        n3_t = load_list("n3_t", n3)
+        n4_t = load_list("n4_t", n4)
+
+        w1_g = group_weight("w1_g", w1_raw, [(on_vector, 0, 64), (on_scalar, 64, 128)])
+        xs = new("xs", [P, S], U8)
+        nc.vector.tensor_copy(xs[:], xs_all[:].indirect(offs_t[:]))
+        w1_q = quantize("w1", w1_g)
+        xw = new("xw", [P, S], U32)
+        nc.vector.tensor_copy(xw[:], xw_all[:].bitcast(U32).indirect(offs_t[:]))
+
+        y_bank = [psum.tile([P, S], F32, name="y_bank%d" % t) for t in tiles]
+        y_win = [new("y_win%d" % t, [P, WIN], F32) for t in tiles]
+        ex_win = [new("ex_win%d" % t, [P, WIN], F32) for t in tiles]
+        ex_own = [new("ex_own%d" % t, [P, S], F32) for t in tiles]
+        for t in tiles:
+            product(y_bank[t], w1_q, t, (xw, xs), True, True)
+        for t in tiles:
+            nc.scalar.activation(ex_win[t][:, :S], y_bank[t][:], ACT.Exp)
+            nc.sync.dma_start(ex_own[t][:], ex_win[t][:, :S])
+        for t in tiles:
+            (on_vector if t < 2 else on_scalar)(y_win[t][:, :S], y_bank[t][:])
+
+        w2_q = quantize("w2", group_weight("w2_g", w2_raw, [(on_vector, 0, 128)]))
+        w3_q = quantize("w3", group_weight("w3_g", w3_raw, [(on_vector, 0, 128)]))
+        neg_gm = new("neg_gm", [P, PACK], F32)
+        nc.vector.tensor_scalar(neg_gm[:], gm_t[:], -1.0, None, ALU.mult)
+
+        gate = [new("gate%d" % t, [P, S], F32) for t in tiles]
+        for t in tiles:
+            nc.scalar.activation(gate[t][:], y_win[t][:].indirect(n1_t[:]), ACT.Sigmoid)
+        total = [new("total%d" % t, [P, S], F32) for t in tiles]
+        for t in tiles:
+            nc.vector.tensor_tensor(total[t][:], ex_win[t][:].indirect(n2_t[:]), ex_own[t][:], ALU.add)
+        z = new("z", [P, PACK, S], BF16)
+        for t in tiles:
+            nc.vector.scalar_tensor_tensor(z[:, t, :], y_bank[t][:], gn_t[:, t : t + 1], gate[t][:], ALU.mult, ALU.mult)
+        for t in tiles:
+            nc.scalar.activation(total[t][:], total[t][:], ACT.Ln)
+        diff = [new("diff%d" % t, [P, S], F32) for t in tiles]
+        z2 = new("z2", [P, PACK, S], BF16)
+        z_g = group_values("z_g", z, [(on_vector, 0, 64), (on_scalar, 64, 128)])
+        for t in tiles:
+            nc.vector.tensor_tensor(diff[t][:], y_win[t][:].indirect(n3_t[:]), total[t][:], ALU.subtract)
+            if t < last:
+                nc.scalar.activation(z2[:, t, :], diff[t][:], ACT.Copy, scale=neg_gm[:, t : t + 1])
+        z_q = quantize("z", z_g)
+        nc.vector.tensor_scalar(z2[:, last, :], diff[last][:], neg_gm[:, last:], None, ALU.mult)
+        h_bank = [psum.tile([P, S], F32, name="h_bank%d" % t) for t in tiles]
+        for t in tiles:
+            product(h_bank[t], w2_q, t, z_q, True, False)
+        z2_g = group_values("z2_g", z2, [(on_vector, 0, 88), (on_scalar, 88, 128)])
+        z2_q = quantize("z2", z2_g)
+        for t in tiles:
+            product(h_bank[t], w3_q, t, z2_q, False, True)
+
+        warm = new("warm", [P, 1], F32)
+        nc.scalar.activation(warm[:], z2_g[:, PACK * S - 1 :], ACT.Abs_reciprocal_sqrt, bias=0.5, scale=0.0)
+        h_win = [new("h_win%d" % t, [P, WIN], F32) for t in tiles]
+        hh = [new("hh%d" % t, [P, S], F32) for t in tiles]
+        pa = [new("pa%d" % t, [P, S], F32) for t in tiles]
+        pp = [new("pp%d" % t, [P, S], F32) for t in tiles]
+        den = [new("den%d" % t, [P, S], F32) for t in tiles]
+        rows = out.rearrange("(p t) s -> p t s", t=PACK)
+        num = pp
+
+        def fetch(t):
+            nc.scalar.copy(h_win[t][:, :S], h_bank[t][:])
+            nc.vector.tensor_copy(pa[t][:], h_win[t][:].indirect(n4_t[:]))
+            nc.scalar.activation(hh[t][:], h_bank[t][:], ACT.Square)
+
+        def denominator(t):
+            nc.scalar.activation(pp[t][:], pa[t][:], ACT.Square)
+            nc.vector.tensor_tensor(den[t][:], pp[t][:], hh[t][:], ALU.add)
+            nc.vector.scalar_tensor_tensor(num[t][:], h_bank[t][:], 2.0, pa[t][:], ALU.mult, ALU.mult)
+            nc.scalar.activation(den[t][:], den[t][:], ACT.Abs_reciprocal_sqrt, bias=0.5)
+
+        def finish(t):
+            nc.scalar.activation(den[t][:], den[t][:], ACT.Square)
+            nc.vector.tensor_tensor(num[t][:], num[t][:], den[t][:], ALU.mult)
+            nc.sync.dma_start(rows[:, t, :], num[t][:])
+
+        for step in range(PACK + 2):
+            if step < PACK:
+                fetch(step)
+            if 1 <= step <= PACK:
+                denominator(step - 1)
+            if step >= 2:
+                finish(step - 2)

@@ -18,6 +18,7 @@ ALU = mybir.AluOpType
 P = 128
 PACK = 4
 WIN = 2 * S
+HALF = S // 2
 
 
 def tile_picked_joingatelseharm_none_p_kernel(tc, x_words, x_scales, w1, gn, gm, w2, w3, offs, n1, n2, n3, n4, out):
@@ -26,8 +27,8 @@ def tile_picked_joingatelseharm_none_p_kernel(tc, x_words, x_scales, w1, gn, gm,
         keep = ctx.enter_context(tc.tile_pool(name="keep", bufs=1))
         psum = ctx.enter_context(tc.psum_pool(name="psum", bufs=1))
 
-        def new(name, shape, dtype):
-            return keep.tile(shape, dtype, name=name, align_bytes=64)
+        def new(name, shape, dtype, tag=None):
+            return keep.tile(shape, dtype, name=name, tag=tag or name, align_bytes=64)
 
         def load_list(name, src):
             dst = keep.tile([P, S // 16], U16, name=name)
@@ -60,8 +61,8 @@ def tile_picked_joingatelseharm_none_p_kernel(tc, x_words, x_scales, w1, gn, gm,
                 copy(dst[:, lo:hi], src[:, lo:hi])
             return grouped
 
-        def quantize(name, grouped):
-            codes = new(name + "_codes", [P, 512], U32)
+        def quantize(name, grouped, codes_tag=None):
+            codes = new(name + "_codes", [P, 512], U32, codes_tag)
             scales = new(name + "_scales", [P, 512], U8)
             nc.vector.quantize_mx(out=codes[:].bitcast(FP8X4), scales=scales[:], in_=grouped[:])
             return codes, scales
@@ -83,13 +84,13 @@ def tile_picked_joingatelseharm_none_p_kernel(tc, x_words, x_scales, w1, gn, gm,
         nc.vector.memset(xs_all[:].bitcast(I32), 0)
         w1_raw = load_weight("w1_raw", w1)
         offs_t = load_list("offs_t", offs)
+        n2_t = load_list("n2_t", n2)
         for q in range(4):
             nc.sync.dma_start(xs_all[32 * q : 32 * q + 4, :].bitcast(I32), x_scales[0, 4 * q : 4 * q + 4, :].bitcast(I32))
         xw_all = new("xw_all", [P, T], I32)
         nc.sync.dma_start(xw_all[:], x_words[0].rearrange("p n r -> p (n r)").bitcast(I32))
         w2_raw = load_weight("w2_raw", w2)
         w3_raw = load_weight("w3_raw", w3)
-        n2_t = load_list("n2_t", n2)
         n1_t = load_list("n1_t", n1)
         gn_t = load_gain("gn_t", gn)
         gm_t = load_gain("gm_t", gm)
@@ -99,85 +100,107 @@ def tile_picked_joingatelseharm_none_p_kernel(tc, x_words, x_scales, w1, gn, gm,
         w1_g = group_weight("w1_g", w1_raw, [(on_vector, 0, 64), (on_scalar, 64, 128)])
         xs = new("xs", [P, S], U8)
         nc.vector.tensor_copy(xs[:], xs_all[:].indirect(offs_t[:]))
-        w1_q = quantize("w1", w1_g)
+        w1_q = quantize("w1", w1_g, "xs_all")
         xw = new("xw", [P, S], U32)
-        nc.vector.tensor_copy(xw[:], xw_all[:].bitcast(U32).indirect(offs_t[:]))
+        for half in range(2):
+            nc.vector.tensor_copy(xw[:, half * HALF : (half + 1) * HALF], xw_all[:].bitcast(U32).indirect(offs_t[:, half * 16 : (half + 1) * 16]))
 
         y_bank = [psum.tile([P, S], F32, name="y_bank%d" % t) for t in tiles]
         y_win = [new("y_win%d" % t, [P, WIN], F32) for t in tiles]
         ex_win = [new("ex_win%d" % t, [P, WIN], F32) for t in tiles]
         ex_own = [new("ex_own%d" % t, [P, S], F32) for t in tiles]
+        gate = new("gate", [P, PACK, S], F32)
+        own_halves = [gate[:, 0, :HALF], ex_own[2][:, HALF:]]
         for t in tiles:
-            product(y_bank[t], w1_q, t, (xw, xs), True, True)
+            for half in range(2):
+                cols = slice(half * HALF, (half + 1) * HALF)
+                product(y_bank[t][:, cols], w1_q, t, (xw[:, cols], xs[:, cols]), True, True)
         for t in tiles:
             nc.scalar.activation(ex_win[t][:, :S], y_bank[t][:], ACT.Exp)
-            nc.sync.dma_start(ex_own[t][:], ex_win[t][:, :S])
-        for t in tiles:
-            (on_vector if t < 2 else on_scalar)(y_win[t][:, :S], y_bank[t][:])
+            if t < 2:
+                nc.sync.dma_start(ex_own[t][:], ex_win[t][:, :S])
+            elif t == 2:
+                for half in range(2):
+                    nc.sync.dma_start(own_halves[half], ex_win[t][:, half * HALF : (half + 1) * HALF])
+        for t in reversed(tiles):
+            (on_vector if t < 0 else on_scalar)(y_win[t][:, :S], y_bank[t][:])
 
+        nc.scalar.activation(ex_own[last][:], y_win[last][:].indirect(n2_t[:]), ACT.Exp)
         w2_q = quantize("w2", group_weight("w2_g", w2_raw, [(on_vector, 0, 128)]))
         w3_q = quantize("w3", group_weight("w3_g", w3_raw, [(on_vector, 0, 128)]))
-        neg_gm = new("neg_gm", [P, PACK], F32)
-        nc.vector.tensor_scalar(neg_gm[:], gm_t[:], -1.0, None, ALU.mult)
 
-        gate = [new("gate%d" % t, [P, S], F32) for t in tiles]
-        for t in tiles:
-            nc.scalar.activation(gate[t][:], y_win[t][:].indirect(n1_t[:]), ACT.Sigmoid)
+        middle = gate[:, :, 192 : 192 + P]
+        straddle = gate[:].rearrange("p (a b) s -> p a (b s)", a=2)[:, :, S - P : S + P]
         total = [new("total%d" % t, [P, S], F32) for t in tiles]
         for t in tiles:
-            nc.vector.tensor_tensor(total[t][:], ex_win[t][:].indirect(n2_t[:]), ex_own[t][:], ALU.add)
-        z = new("z", [P, PACK, S], BF16)
-        for t in tiles:
-            nc.vector.scalar_tensor_tensor(z[:, t, :], y_bank[t][:], gn_t[:, t : t + 1], gate[t][:], ALU.mult, ALU.mult)
-        for t in tiles:
-            nc.scalar.activation(total[t][:], total[t][:], ACT.Ln)
-        diff = [new("diff%d" % t, [P, S], F32) for t in tiles]
-        z2 = new("z2", [P, PACK, S], BF16)
-        z_g = group_values("z_g", z, [(on_vector, 0, 64), (on_scalar, 64, 128)])
+            if t < 2:
+                nc.vector.tensor_tensor(total[t][:], ex_win[t][:].indirect(n2_t[:]), ex_own[t][:], ALU.add)
+                nc.scalar.activation(total[t][:], total[t][:], ACT.Ln)
+            elif t == 2:
+                for half in range(2):
+                    nc.vector.tensor_tensor(straddle[:, half, :], ex_win[t][:].indirect(n2_t[:, half * HALF // 16 : (half + 1) * HALF // 16]), own_halves[half], ALU.add)
+                nc.scalar.activation(total[t][:].rearrange("p (a b) -> p a b", a=2), straddle, ACT.Ln)
+            else:
+                nc.vector.tensor_tensor(middle, ex_win[t][:, :S].rearrange(quarters, a=PACK), ex_own[t][:].rearrange(quarters, a=PACK), ALU.add)
+                nc.scalar.activation(total[t][:].rearrange(quarters, a=PACK), middle, ACT.Ln)
+        diff = [ex_own[2], ex_own[last]] + [new("diff%d" % t, [P, S], F32) for t in range(2, PACK)]
         for t in tiles:
             nc.vector.tensor_tensor(diff[t][:], y_win[t][:].indirect(n3_t[:]), total[t][:], ALU.subtract)
-            if t < last:
-                nc.scalar.activation(z2[:, t, :], diff[t][:], ACT.Copy, scale=neg_gm[:, t : t + 1])
-        z_q = quantize("z", z_g)
-        nc.vector.tensor_scalar(z2[:, last, :], diff[last][:], neg_gm[:, last:], None, ALU.mult)
-        h_bank = [psum.tile([P, S], F32, name="h_bank%d" % t) for t in tiles]
         for t in tiles:
-            product(h_bank[t], w2_q, t, z_q, True, False)
-        z2_g = group_values("z2_g", z2, [(on_vector, 0, 88), (on_scalar, 88, 128)])
+            nc.scalar.activation(gate[:, t, :], y_win[t][:].indirect(n1_t[:]), ACT.Sigmoid)
+        z = new("z", [P, PACK, S], BF16)
+        z2 = new("z2", [P, PACK, S], BF16)
+        for t in tiles:
+            nc.vector.tensor_scalar(z2[:, t, :], diff[t][:], gm_t[:, t : t + 1], -1.0, ALU.mult, ALU.mult)
+        for t in tiles:
+            nc.vector.scalar_tensor_tensor(z[:, t, :], y_bank[t][:], gn_t[:, t : t + 1], gate[:, t, :], ALU.mult, ALU.mult)
+        z2_g = group_values("z2_g", z2, [(on_scalar, 0, 128)])
+        z_g = group_values("z_g", z, [(on_vector, 0, 80), (on_scalar, 80, 128)])
+        z_q = (new("z_codes", [P, S], U32), new("z_scales", [P, S], U8))
         z2_q = quantize("z2", z2_g)
-        for t in tiles:
+        lo, hi = slice(0, HALF), slice(HALF, S)
+
+        def quantize_half(quantized, grouped, cols):
+            nc.vector.quantize_mx(out=quantized[0][:, cols].bitcast(FP8X4), scales=quantized[1][:, cols], in_=grouped[:, PACK * cols.start : PACK * cols.stop])
+
+        def half_of(quantized, cols):
+            return (quantized[0][:, cols], quantized[1][:, cols])
+
+        quantize_half(z_q, z_g, lo)
+        quantize_half(z_q, z_g, hi)
+        h_bank = [psum.tile([P, S], F32, name="h_bank%d" % t) for t in tiles]
+        for cols in (lo, hi):
+            product(h_bank[0][:, cols], w3_q, 0, half_of(z2_q, cols), True, False)
+            product(h_bank[0][:, cols], w2_q, 0, half_of(z_q, cols), False, True)
+        for t in range(1, PACK):
+            product(h_bank[t], w2_q, t, z_q, True, False)
             product(h_bank[t], w3_q, t, z2_q, False, True)
 
         warm = new("warm", [P, 1], F32)
-        nc.scalar.activation(warm[:], z2_g[:, PACK * S - 1 :], ACT.Abs_reciprocal_sqrt, bias=0.5, scale=0.0)
+        nc.scalar.activation(warm[:], z_g[:, PACK * S - 1 :], ACT.Abs_reciprocal_sqrt, bias=0.5, scale=0.0)
         h_win = [new("h_win%d" % t, [P, WIN], F32) for t in tiles]
         hh = [new("hh%d" % t, [P, S], F32) for t in tiles]
         pa = [new("pa%d" % t, [P, S], F32) for t in tiles]
-        pp = [new("pp%d" % t, [P, S], F32) for t in tiles]
+        pp = [new("pp%d" % t, [P, S], F32) for t in range(last)]
         den = [new("den%d" % t, [P, S], F32) for t in tiles]
+        num = new("num", [P, PACK, S], F32)
         rows = out.rearrange("(p t) s -> p t s", t=PACK)
-        num = pp
-
-        def fetch(t):
+        for t in tiles:
             nc.scalar.copy(h_win[t][:, :S], h_bank[t][:])
             nc.vector.tensor_copy(pa[t][:], h_win[t][:].indirect(n4_t[:]))
+        for t in tiles:
             nc.scalar.activation(hh[t][:], h_bank[t][:], ACT.Square)
-
-        def denominator(t):
-            nc.scalar.activation(pp[t][:], pa[t][:], ACT.Square)
-            nc.vector.tensor_tensor(den[t][:], pp[t][:], hh[t][:], ALU.add)
-            nc.vector.scalar_tensor_tensor(num[t][:], h_bank[t][:], 2.0, pa[t][:], ALU.mult, ALU.mult)
+            if t < last:
+                nc.scalar.activation(pp[t][:], pa[t][:], ACT.Square)
+                nc.vector.tensor_tensor(den[t][:], pp[t][:], hh[t][:], ALU.add)
+            else:
+                nc.scalar.activation(num[:, :, :P], pa[t][:].rearrange(quarters, a=PACK), ACT.Square)
+                nc.vector.tensor_tensor(den[t][:].rearrange(quarters, a=PACK), num[:, :, :P], hh[t][:].rearrange(quarters, a=PACK), ALU.add)
+        for t in tiles:
             nc.scalar.activation(den[t][:], den[t][:], ACT.Abs_reciprocal_sqrt, bias=0.5)
-
-        def finish(t):
             nc.scalar.activation(den[t][:], den[t][:], ACT.Square)
-            nc.vector.tensor_tensor(num[t][:], num[t][:], den[t][:], ALU.mult)
-            nc.sync.dma_start(rows[:, t, :], num[t][:])
-
-        for step in range(PACK + 2):
-            if step < PACK:
-                fetch(step)
-            if 1 <= step <= PACK:
-                denominator(step - 1)
-            if step >= 2:
-                finish(step - 2)
+            nc.vector.scalar_tensor_tensor(num[:, t, :], h_bank[t][:], 2.0, pa[t][:], ALU.mult, ALU.mult)
+        for t in tiles:
+            for cols in (slice(0, S),) if t < last else (slice(0, HALF), slice(HALF, S)):
+                nc.vector.tensor_tensor(num[:, t, cols], num[:, t, cols], den[t][:, cols], ALU.mult)
+                nc.sync.dma_start(rows[:, t, cols], num[:, t, cols])

@@ -1,6 +1,7 @@
 from contextlib import ExitStack
 
 import concourse.mybir as mybir
+from concourse.masks import make_identity
 
 K, T, S, N, H = 512, 2048, 512, 512, 512
 FLOPS = 2 * K * H * S + 2 * 2 * H * N * S
@@ -80,6 +81,8 @@ def tile_picked_joingatelseharm_none_p_kernel(tc, x_words, x_scales, w1, gn, gm,
         last = PACK - 1
         quarters = "p (a b) -> p a b"
 
+        identity = new("identity", [P, P], F32)
+        make_identity(nc, identity[:])
         xs_all = new("xs_all", [P, T], U8)
         nc.vector.memset(xs_all[:].bitcast(I32), 0)
         w1_raw = load_weight("w1_raw", w1)
@@ -154,8 +157,8 @@ def tile_picked_joingatelseharm_none_p_kernel(tc, x_words, x_scales, w1, gn, gm,
             nc.vector.tensor_scalar(z2[:, t, :], diff[t][:], gm_t[:, t : t + 1], -1.0, ALU.mult, ALU.mult)
         for t in tiles:
             nc.vector.scalar_tensor_tensor(z[:, t, :], y_bank[t][:], gn_t[:, t : t + 1], gate[:, t, :], ALU.mult, ALU.mult)
-        z2_g = group_values("z2_g", z2, [(on_scalar, 0, 128)])
-        z_g = group_values("z_g", z, [(on_vector, 0, 80), (on_scalar, 80, 128)])
+        z2_g = group_values("z2_g", z2, [(on_vector, 0, 32), (on_scalar, 32, 128)])
+        z_g = group_values("z_g", z, [(on_vector, 0, 104), (on_scalar, 104, 128)])
         z_q = (new("z_codes", [P, S], U32), new("z_scales", [P, S], U8))
         z2_q = quantize("z2", z2_g)
         lo, hi = slice(0, HALF), slice(HALF, S)
@@ -178,29 +181,64 @@ def tile_picked_joingatelseharm_none_p_kernel(tc, x_words, x_scales, w1, gn, gm,
 
         warm = new("warm", [P, 1], F32)
         nc.scalar.activation(warm[:], z_g[:, PACK * S - 1 :], ACT.Abs_reciprocal_sqrt, bias=0.5, scale=0.0)
-        h_win = [new("h_win%d" % t, [P, WIN], F32) for t in tiles]
+        h_win = [new("h_win%d" % t, [P, WIN if t < last else PACK * S], F32) for t in tiles]
+        twice_last = new("twice_last", [P, S], F32)
+        twice = [h_win[last][:, (t + 1) * S : (t + 2) * S] for t in range(last)] + [twice_last[:]]
         hh = [new("hh%d" % t, [P, S], F32) for t in tiles]
         pa = [new("pa%d" % t, [P, S], F32) for t in tiles]
-        pp = [new("pp%d" % t, [P, S], F32) for t in range(last)]
+        pp = [new("pp%d" % t, [P, S], F32) for t in tiles]
         den = [new("den%d" % t, [P, S], F32) for t in tiles]
         num = new("num", [P, PACK, S], F32)
         rows = out.rearrange("(p t) s -> p t s", t=PACK)
-        for t in tiles:
+        blocks = [slice(b * P, (b + 1) * P) for b in range(S // P)]
+        factor = {}
+
+        def fetch(t):
             nc.scalar.copy(h_win[t][:, :S], h_bank[t][:])
             nc.vector.tensor_copy(pa[t][:], h_win[t][:].indirect(n4_t[:]))
-        for t in tiles:
-            nc.scalar.activation(hh[t][:], h_bank[t][:], ACT.Square)
-            if t < last:
-                nc.scalar.activation(pp[t][:], pa[t][:], ACT.Square)
-                nc.vector.tensor_tensor(den[t][:], pp[t][:], hh[t][:], ALU.add)
+
+        def own_square(t):
+            if t in ():
+                nc.vector.tensor_tensor(hh[t][:], h_bank[t][:], h_win[t][:, :S], ALU.mult)
             else:
-                nc.scalar.activation(num[:, :, :P], pa[t][:].rearrange(quarters, a=PACK), ACT.Square)
-                nc.vector.tensor_tensor(den[t][:].rearrange(quarters, a=PACK), num[:, :, :P], hh[t][:].rearrange(quarters, a=PACK), ALU.add)
+                nc.scalar.activation(hh[t][:], h_bank[t][:], ACT.Square)
+
+        def fetched_square(t):
+            if t in (3,):
+                nc.vector.tensor_tensor(pp[t][:], pa[t][:], pa[t][:], ALU.mult)
+            else:
+                nc.scalar.activation(pp[t][:], pa[t][:], ACT.Square)
+
+        def inverse(t):
+            if t < last:
+                turned = psum.tile([P, S], F32, name="turned%d" % t, tag="y_bank%d" % t)
+                for cols in blocks:
+                    nc.tensor.matmul(turned[:, cols], hh[t][:, cols], identity[:], start=True, stop=False, is_transpose=True)
+                    nc.tensor.matmul(turned[:, cols], pp[t][:, cols], identity[:], start=False, stop=True, is_transpose=True)
+                nc.scalar.activation(den[t][:], turned[:], ACT.Abs_reciprocal_sqrt, bias=0.5)
+                nc.scalar.activation(den[t][:], den[t][:], ACT.Square)
+                back = psum.tile([P, S], F32, name="back%d" % t, tag="y_bank%d" % t)
+                for cols in blocks:
+                    nc.tensor.transpose(back[:, cols], den[t][:, cols], identity[:])
+                factor[t] = back
+            else:
+                nc.vector.tensor_tensor(den[t][:], pp[t][:], hh[t][:], ALU.add)
+                nc.scalar.activation(den[t][:], den[t][:], ACT.Abs_reciprocal_sqrt, bias=0.5)
+                nc.scalar.activation(den[t][:], den[t][:], ACT.Square)
+                factor[t] = den[t]
+
         for t in tiles:
-            nc.scalar.activation(den[t][:], den[t][:], ACT.Abs_reciprocal_sqrt, bias=0.5)
-            nc.scalar.activation(den[t][:], den[t][:], ACT.Square)
-            nc.vector.scalar_tensor_tensor(num[:, t, :], h_bank[t][:], 2.0, pa[t][:], ALU.mult, ALU.mult)
+            fetch(t)
+            if t >= 2:
+                fetched_square(t - 2)
+            own_square(t)
+        fetched_square(2)
+        fetched_square(3)
         for t in tiles:
-            for cols in (slice(0, S),) if t < last else (slice(0, HALF), slice(HALF, S)):
-                nc.vector.tensor_tensor(num[:, t, cols], num[:, t, cols], den[t][:, cols], ALU.mult)
+            inverse(t)
+        for t in tiles:
+            nc.vector.scalar_tensor_tensor(twice[t][:], h_bank[t][:], 2.0, pa[t][:], ALU.mult, ALU.mult)
+        for t in tiles:
+            for cols in (slice(0, S),) if t != last else (lo, hi):
+                nc.vector.tensor_tensor(num[:, t, cols], factor[t][:, cols], twice[t][:, cols], ALU.mult)
                 nc.sync.dma_start(rows[:, t, cols], num[:, t, cols])

from contextlib import ExitStack

import concourse.mybir as mybir
from concourse.masks import make_identity

K, T, S, N, H = 512, 2048, 512, 512, 512
FLOPS = 2 * K * H * S + 2 * 2 * H * N * S

F32 = mybir.dt.float32
BF16 = mybir.dt.bfloat16
I32 = mybir.dt.int32
U32 = mybir.dt.uint32
U16 = mybir.dt.uint16
U8 = mybir.dt.uint8
FP8X4 = mybir.dt.float8_e4m3fn_x4
ACT = mybir.ActivationFunctionType
ALU = mybir.AluOpType

P = 128
PACK = 4
WIN = 2 * S
HALF = S // 2


def tile_picked_joingatelseharm_none_p_kernel(tc, x_words, x_scales, w1, gn, gm, w2, w3, offs, n1, n2, n3, n4, out):
    nc = tc.nc
    with ExitStack() as ctx:
        keep = ctx.enter_context(tc.tile_pool(name="keep", bufs=1))
        psum = ctx.enter_context(tc.psum_pool(name="psum", bufs=1))

        def new(name, shape, dtype, tag=None):
            return keep.tile(shape, dtype, name=name, tag=tag or name, align_bytes=64)

        def load_list(name, src):
            dst = keep.tile([P, S // 16], U16, name=name)
            nc.sync.dma_start(dst[:], src)
            return dst

        def load_weight(name, w):
            raw = new(name, [P, PACK, 512], F32)
            nc.sync.dma_start(raw[:], w.rearrange("(p j) c -> p j c", j=PACK))
            return raw

        def load_gain(name, g):
            dst = new(name, [P, PACK], F32)
            nc.sync.dma_start(dst[:], g.rearrange("(p t) o -> p (t o)", t=PACK))
            return dst

        def group_weight(name, raw, shares):
            grouped = new(name, [P, PACK * 512], BF16)
            dst = grouped[:].rearrange("p (t m j) -> p m j t", t=PACK, j=PACK)
            src = raw[:].rearrange("p j (m t) -> p m j t", t=PACK)
            for copy, lo, hi in shares:
                copy(dst[:, lo:hi], src[:, lo:hi])
            return grouped

        def group_values(name, planes, shares):
            grouped = new(name, [P, PACK * S], BF16)
            dst = grouped[:].rearrange("p (c i t) -> p c t i", t=PACK, i=4)
            src = planes[:].rearrange("p t (c i) -> p c t i", i=4)
            for copy, lo, hi in shares:
                copy(dst[:, lo:hi], src[:, lo:hi])
            return grouped

        def quantize(name, grouped, codes_tag=None):
            codes = new(name + "_codes", [P, 512], U32, codes_tag)
            scales = new(name + "_scales", [P, 512], U8)
            nc.vector.quantize_mx(out=codes[:].bitcast(FP8X4), scales=scales[:], in_=grouped[:])
            return codes, scales

        def product(bank, weight, t, moving, start, stop):
            cols = slice(t * P, (t + 1) * P)
            nc.tensor.matmul_mx(
                out=bank[:], lhsT=weight[0][:, cols].bitcast(FP8X4), lhsT_scale=weight[1][:, cols],
                rhs=moving[0][:].bitcast(FP8X4), rhs_scale=moving[1][:], start=start, stop=stop,
            )

        tiles = range(PACK)

        on_vector, on_scalar = nc.vector.tensor_copy, nc.scalar.copy
        last = PACK - 1
        quarters = "p (a b) -> p a b"

        identity = new("identity", [P, P], F32)
        make_identity(nc, identity[:])
        xs_all = new("xs_all", [P, T], U8)
        nc.vector.memset(xs_all[:].bitcast(I32), 0)
        w1_raw = load_weight("w1_raw", w1)
        offs_t = load_list("offs_t", offs)
        n2_t = load_list("n2_t", n2)
        for q in range(4):
            nc.sync.dma_start(xs_all[32 * q : 32 * q + 4, :].bitcast(I32), x_scales[0, 4 * q : 4 * q + 4, :].bitcast(I32))
        xw_all = new("xw_all", [P, T], I32)
        nc.sync.dma_start(xw_all[:], x_words[0].rearrange("p n r -> p (n r)").bitcast(I32))
        w2_raw = load_weight("w2_raw", w2)
        w3_raw = load_weight("w3_raw", w3)
        n1_t = load_list("n1_t", n1)
        gn_t = load_gain("gn_t", gn)
        gm_t = load_gain("gm_t", gm)
        n3_t = load_list("n3_t", n3)
        n4_t = load_list("n4_t", n4)

        w1_g = group_weight("w1_g", w1_raw, [(on_vector, 0, 64), (on_scalar, 64, 128)])
        xs = new("xs", [P, S], U8)
        nc.vector.tensor_copy(xs[:], xs_all[:].indirect(offs_t[:]))
        w1_q = quantize("w1", w1_g, "xs_all")
        xw = new("xw", [P, S], U32)
        for half in range(2):
            nc.vector.tensor_copy(xw[:, half * HALF : (half + 1) * HALF], xw_all[:].bitcast(U32).indirect(offs_t[:, half * 16 : (half + 1) * 16]))

        y_bank = [psum.tile([P, S], F32, name="y_bank%d" % t) for t in tiles]
        y_win = [new("y_win%d" % t, [P, WIN], F32) for t in tiles]
        ex_win = [new("ex_win%d" % t, [P, WIN], F32) for t in tiles]
        ex_own = [new("ex_own%d" % t, [P, S], F32) for t in tiles]
        gate = new("gate", [P, PACK, S], F32)
        own_halves = [gate[:, 0, :HALF], ex_own[2][:, HALF:]]
        for t in tiles:
            for half in range(2):
                cols = slice(half * HALF, (half + 1) * HALF)
                product(y_bank[t][:, cols], w1_q, t, (xw[:, cols], xs[:, cols]), True, True)
        for t in tiles:
            nc.scalar.activation(ex_win[t][:, :S], y_bank[t][:], ACT.Exp)
            if t < 2:
                nc.sync.dma_start(ex_own[t][:], ex_win[t][:, :S])
            elif t == 2:
                for half in range(2):
                    nc.sync.dma_start(own_halves[half], ex_win[t][:, half * HALF : (half + 1) * HALF])
        for t in reversed(tiles):
            (on_vector if t < 0 else on_scalar)(y_win[t][:, :S], y_bank[t][:])

        nc.scalar.activation(ex_own[last][:], y_win[last][:].indirect(n2_t[:]), ACT.Exp)
        w2_q = quantize("w2", group_weight("w2_g", w2_raw, [(on_vector, 0, 128)]))
        w3_q = quantize("w3", group_weight("w3_g", w3_raw, [(on_vector, 0, 128)]))

        middle = gate[:, :, 192 : 192 + P]
        straddle = gate[:].rearrange("p (a b) s -> p a (b s)", a=2)[:, :, S - P : S + P]
        total = [new("total%d" % t, [P, S], F32) for t in tiles]
        for t in tiles:
            if t < 2:
                nc.vector.tensor_tensor(total[t][:], ex_win[t][:].indirect(n2_t[:]), ex_own[t][:], ALU.add)
                nc.scalar.activation(total[t][:], total[t][:], ACT.Ln)
            elif t == 2:
                for half in range(2):
                    nc.vector.tensor_tensor(straddle[:, half, :], ex_win[t][:].indirect(n2_t[:, half * HALF // 16 : (half + 1) * HALF // 16]), own_halves[half], ALU.add)
                nc.scalar.activation(total[t][:].rearrange("p (a b) -> p a b", a=2), straddle, ACT.Ln)
            else:
                nc.vector.tensor_tensor(middle, ex_win[t][:, :S].rearrange(quarters, a=PACK), ex_own[t][:].rearrange(quarters, a=PACK), ALU.add)
                nc.scalar.activation(total[t][:].rearrange(quarters, a=PACK), middle, ACT.Ln)
        diff = [ex_own[2], ex_own[last]] + [new("diff%d" % t, [P, S], F32) for t in range(2, PACK)]
        for t in tiles:
            nc.vector.tensor_tensor(diff[t][:], y_win[t][:].indirect(n3_t[:]), total[t][:], ALU.subtract)
        for t in tiles:
            nc.scalar.activation(gate[:, t, :], y_win[t][:].indirect(n1_t[:]), ACT.Sigmoid)
        z = new("z", [P, PACK, S], BF16)
        z2 = new("z2", [P, PACK, S], BF16)
        for t in tiles:
            nc.vector.tensor_scalar(z2[:, t, :], diff[t][:], gm_t[:, t : t + 1], -1.0, ALU.mult, ALU.mult)
        for t in tiles:
            nc.vector.scalar_tensor_tensor(z[:, t, :], y_bank[t][:], gn_t[:, t : t + 1], gate[:, t, :], ALU.mult, ALU.mult)
        z2_g = group_values("z2_g", z2, [(on_vector, 0, 32), (on_scalar, 32, 128)])
        z_g = group_values("z_g", z, [(on_vector, 0, 104), (on_scalar, 104, 128)])
        z_q = (new("z_codes", [P, S], U32), new("z_scales", [P, S], U8))
        z2_q = quantize("z2", z2_g)
        lo, hi = slice(0, HALF), slice(HALF, S)

        def quantize_half(quantized, grouped, cols):
            nc.vector.quantize_mx(out=quantized[0][:, cols].bitcast(FP8X4), scales=quantized[1][:, cols], in_=grouped[:, PACK * cols.start : PACK * cols.stop])

        def half_of(quantized, cols):
            return (quantized[0][:, cols], quantized[1][:, cols])

        quantize_half(z_q, z_g, lo)
        quantize_half(z_q, z_g, hi)
        h_bank = [psum.tile([P, S], F32, name="h_bank%d" % t) for t in tiles]
        for cols in (lo, hi):
            product(h_bank[0][:, cols], w3_q, 0, half_of(z2_q, cols), True, False)
            product(h_bank[0][:, cols], w2_q, 0, half_of(z_q, cols), False, True)
        for t in range(1, PACK):
            product(h_bank[t], w2_q, t, z_q, True, False)
            product(h_bank[t], w3_q, t, z2_q, False, True)

        warm = new("warm", [P, 1], F32)
        nc.scalar.activation(warm[:], z_g[:, PACK * S - 1 :], ACT.Abs_reciprocal_sqrt, bias=0.5, scale=0.0)
        h_win = [new("h_win%d" % t, [P, WIN if t < last else PACK * S], F32) for t in tiles]
        twice_last = new("twice_last", [P, S], F32)
        twice = [h_win[last][:, (t + 1) * S : (t + 2) * S] for t in range(last)] + [twice_last[:]]
        hh = [new("hh%d" % t, [P, S], F32) for t in tiles]
        pa = [new("pa%d" % t, [P, S], F32) for t in tiles]
        pp = [new("pp%d" % t, [P, S], F32) for t in tiles]
        den = [new("den%d" % t, [P, S], F32) for t in tiles]
        num = new("num", [P, PACK, S], F32)
        rows = out.rearrange("(p t) s -> p t s", t=PACK)
        blocks = [slice(b * P, (b + 1) * P) for b in range(S // P)]
        factor = {}

        def fetch(t):
            nc.scalar.copy(h_win[t][:, :S], h_bank[t][:])
            nc.vector.tensor_copy(pa[t][:], h_win[t][:].indirect(n4_t[:]))

        def own_square(t):
            if t in ():
                nc.vector.tensor_tensor(hh[t][:], h_bank[t][:], h_win[t][:, :S], ALU.mult)
            else:
                nc.scalar.activation(hh[t][:], h_bank[t][:], ACT.Square)

        def fetched_square(t):
            if t in (3,):
                nc.vector.tensor_tensor(pp[t][:], pa[t][:], pa[t][:], ALU.mult)
            else:
                nc.scalar.activation(pp[t][:], pa[t][:], ACT.Square)

        def inverse(t):
            if t < last:
                turned = psum.tile([P, S], F32, name="turned%d" % t, tag="y_bank%d" % t)
                for cols in blocks:
                    nc.tensor.matmul(turned[:, cols], hh[t][:, cols], identity[:], start=True, stop=False, is_transpose=True)
                    nc.tensor.matmul(turned[:, cols], pp[t][:, cols], identity[:], start=False, stop=True, is_transpose=True)
                nc.scalar.activation(den[t][:], turned[:], ACT.Abs_reciprocal_sqrt, bias=0.5)
                nc.scalar.activation(den[t][:], den[t][:], ACT.Square)
                back = psum.tile([P, S], F32, name="back%d" % t, tag="y_bank%d" % t)
                for cols in blocks:
                    nc.tensor.transpose(back[:, cols], den[t][:, cols], identity[:])
                factor[t] = back
            else:
                nc.vector.tensor_tensor(den[t][:], pp[t][:], hh[t][:], ALU.add)
                nc.scalar.activation(den[t][:], den[t][:], ACT.Abs_reciprocal_sqrt, bias=0.5)
                nc.scalar.activation(den[t][:], den[t][:], ACT.Square)
                factor[t] = den[t]

        for t in tiles:
            fetch(t)
            if t >= 2:
                fetched_square(t - 2)
            own_square(t)
        fetched_square(2)
        fetched_square(3)
        for t in tiles:
            inverse(t)
        for t in tiles:
            nc.vector.scalar_tensor_tensor(twice[t][:], h_bank[t][:], 2.0, pa[t][:], ALU.mult, ALU.mult)
        for t in tiles:
            for cols in (slice(0, S),) if t != last else (lo, hi):
                nc.vector.tensor_tensor(num[:, t, cols], factor[t][:, cols], twice[t][:, cols], ALU.mult)
                nc.sync.dma_start(rows[:, t, cols], num[:, t, cols])
